import numpy as np
import ml_dtypes


def mxq(x, axis, fmt="e4m3"):
    dtype, down = {"e4m3": (ml_dtypes.float8_e4m3fn, 7), "e5m2": (ml_dtypes.float8_e5m2, 14)}[fmt]
    v = np.moveaxis(np.asarray(x, np.float32).astype(ml_dtypes.bfloat16).astype(np.float64), axis, -1)
    blocks = v.reshape(v.shape[:-1] + (-1, 32))
    amax = np.abs(blocks).max(-1, keepdims=True)
    byte = np.maximum(np.where(amax > 0, np.frexp(amax)[1] - 1 + 127, 0) - down, 1)
    scale = np.exp2(byte - 127.0)
    codes = (blocks / scale).astype(np.float32).astype(dtype).astype(np.float64)
    return np.moveaxis((codes * scale).reshape(v.shape), -1, axis)


WIDE = False


def mx_kscale(k):
    if not WIDE:
        return np.ones(k)
    levels = np.array([10, -10, 5, -5, 0])
    if k % 512:
        return np.exp2(np.random.permutation(np.resize(levels, k // 32))).repeat(32)
    a = np.empty((k // 512, 16))
    for p in range(k // 512):
        a[p, :8] = np.random.permutation(np.resize(levels, 8))
        for g in range(8):
            far = levels[np.abs(levels - a[p, g]) >= 10]
            a[p, g + 8] = far[np.random.randint(len(far))]
    return np.exp2(a.ravel()).repeat(32)


BF16 = ml_dtypes.bfloat16


def bf(x):
    return np.asarray(x, np.float32).astype(BF16)


def f64(x):
    return np.asarray(x).astype(np.float64)


E2M1 = np.array([0.0, 0.5, 1.0, 1.5, 2.0, 3.0, 4.0, 6.0, -0.0, -0.5, -1.0, -1.5, -2.0, -3.0, -4.0, -6.0])


def pack_weight(w, fmt):
    k, n = w.shape
    w = f64(bf(w)).reshape(k // 32, 32, n)
    amax = np.abs(w).max(1)
    if fmt == "e4m3":
        byte = np.frexp(amax)[1] - 1 + 127 - 7
    else:
        mant, ex = np.frexp(amax / 6.0)
        byte = np.where(mant > 0.5, ex, ex - 1) + 127
    byte = np.clip(np.where(amax > 0, byte, 1), 1, 254)
    scaled = (w * np.exp2(127.0 - byte)[:, None, :]).reshape(k, n).astype(np.float32)
    by_word = np.ascontiguousarray(scaled.reshape(k // 512, 128, 4, n).transpose(0, 1, 3, 2))
    if fmt == "e4m3":
        words = by_word.astype(ml_dtypes.float8_e4m3fn).view(np.uint8)
    else:
        c = by_word.astype(ml_dtypes.float4_e2m1fn).view(np.uint8) & 0xF
        words = c[..., 0::2] | (c[..., 1::2] << 4)
    return np.ascontiguousarray(words), np.ascontiguousarray(byte.astype(np.uint8).reshape(k // 512, 16, n))


def unpack_weight(words, scales, fmt):
    g, p, n, _ = words.shape
    if fmt == "e4m3":
        vals = np.ascontiguousarray(words).view(ml_dtypes.float8_e4m3fn).astype(np.float64)
    else:
        nib = np.empty((g, p, n, 4), np.uint8)
        nib[..., 0::2] = words & 0xF
        nib[..., 1::2] = words >> 4
        vals = E2M1[nib]
    vals = vals * np.repeat(np.exp2(scales.astype(np.float64) - 127.0), 8, axis=1)[..., None]
    return vals.transpose(0, 1, 3, 2).reshape(g * 512, n)


B, J, K, M = 2048, 512, 1024, 512


def draw0():
    s, t = mx_kscale(J), mx_kscale(K)
    theta = np.random.standard_normal((B, J)) * s
    rho = np.random.standard_normal((B, J)) * 0.5 * s
    a = np.random.standard_normal((J, K)) / np.sqrt(J) / s[:, None]
    d1 = np.random.standard_normal(K) * 0.5
    g = (1.0 + 0.1 * np.random.standard_normal(K)) * t
    wr = np.random.standard_normal((K, M)) / np.sqrt(K) / t[:, None]
    wp = np.random.standard_normal((K, M)) / np.sqrt(K) / t[:, None]
    a_words, a_scales = pack_weight(a, "e4m3")
    wr_words, wr_scales = pack_weight(wr, "e4m3")
    wp_words, wp_scales = pack_weight(wp, "e4m3")
    return {"theta": bf(theta), "rho": bf(rho), "a_words": a_words, "a_scales": a_scales, "d1": bf(d1), "g": bf(g), "wr_words": wr_words, "wr_scales": wr_scales, "wp_words": wp_words, "wp_scales": wp_scales}


def interaction_phase(theta, aq, d1):
    return (mxq(f64(theta), 1, "e4m3") @ aq) + f64(d1)[None, :]


def interaction_modulus(rho, aq, g):
    q = mxq(f64(rho), 1, "e4m3") @ aq
    return np.exp(q) * f64(g)[None, :]


def core(theta, rho, a_words, a_scales, d1, g, wr_words, wr_scales, wp_words, wp_scales):
    aq = unpack_weight(a_words, a_scales, "e4m3")
    psi = interaction_phase(theta, aq, d1)
    m = interaction_modulus(rho, aq, g)
    re = m * np.cos(psi)
    pe = m * np.sin(psi)
    y = (mxq(re, 1, "e4m3") @ unpack_weight(wr_words, wr_scales, "e4m3")) + (mxq(pe, 1, "e4m3") @ unpack_weight(wp_words, wp_scales, "e4m3"))
    return y


def e4m3fn_bytes(y):
    return np.clip(np.asarray(y, np.float64), -448.0, 448.0).astype(np.float32).astype(ml_dtypes.float8_e4m3fn).view(np.uint8)


def e4m3fn_values(b):
    return np.asarray(b, np.uint8).view(ml_dtypes.float8_e4m3fn).astype(np.float64)


def setup_inputs():
    d = draw0()
    x0 = np.asarray(d['theta']).astype(np.float64)
    s = (np.max(np.abs(x0), axis=(0,), keepdims=True) / 448.0).astype(np.float32)
    out = {}
    for k, v in d.items():
        if k == 'theta':
            out['theta_bytes'] = e4m3fn_bytes(x0 / s.astype(np.float64))
            out['theta_scale'] = s
        else:
            out[k] = v
    return out


def reference(theta_bytes, theta_scale, rho, a_words, a_scales, d1, g, wr_words, wr_scales, wp_words, wp_scales):
    return core(e4m3fn_values(theta_bytes) * theta_scale.astype(np.float64), rho, a_words, a_scales, d1, g, wr_words, wr_scales, wp_words, wp_scales)

@@ -1,0 +1,273 @@
+import math
+from contextlib import ExitStack
+
+import concourse.mybir as mybir
+from concourse.masks import make_identity
+
+B, J, K, M = 2048, 512, 1024, 512
+FLOPS = 2 * 2 * B * J * K + 2 * 2 * B * K * M
+
+F32 = mybir.dt.float32
+BF16 = mybir.dt.bfloat16
+FP8 = mybir.dt.float8_e4m3fn
+FP8X4 = mybir.dt.float8_e4m3fn_x4
+I32 = mybir.dt.int32
+U32 = mybir.dt.uint32
+U8 = mybir.dt.uint8
+ALU = mybir.AluOpType
+ACT = mybir.ActivationFunctionType
+
+P = 128
+PI = math.pi
+CH = 512
+NCH = B // CH
+NG = 2 * NCH
+
+
+def tile_eulerinteractionpolarlayer_w8_kernel(
+    tc, theta_bytes, theta_scale, rho, a_words, a_scales, d1, g, wr_words, wr_scales, wp_words, wp_scales, out
+):
+    nc = tc.nc
+    with ExitStack() as ctx:
+        const = ctx.enter_context(tc.tile_pool(name="const", bufs=1))
+        sb = ctx.enter_context(tc.tile_pool(name="sb", bufs=1))
+        ps = ctx.enter_context(tc.psum_pool(name="ps", bufs=1))
+
+        tsc = const.tile([P, J], F32, name="tsc")
+        nc.scalar.dma_start(out=tsc[:], in_=theta_scale.rearrange("o k -> (o k)").partition_broadcast(P))
+        d1_t = const.tile([P, 2, 4], BF16, name="d1_t")
+        g_t = const.tile([P, 2, 4], BF16, name="g_t")
+        nc.scalar.dma_start(out=d1_t[:], in_=d1.rearrange("(h p t) -> p h t", p=P, t=4))
+        nc.scalar.dma_start(out=g_t[:], in_=g.rearrange("(h p t) -> p h t", p=P, t=4))
+
+        ident = const.tile([P, P], F32, name="ident")
+        make_identity(nc, ident[:])
+
+        a_sc_raw = const.tile([P, K], U8, name="a_sc_raw", align_bytes=64)
+        w_sc = const.tile([P, M], U8, name="w_sc", align_bytes=64)
+        nc.vector.memset(a_sc_raw[:].bitcast(I32), 0)
+        nc.vector.memset(w_sc[:].bitcast(I32), 0)
+
+        rho_v = rho.rearrange("(c p r) k -> c p r k", p=P, r=4)
+        th_v = theta_bytes.rearrange("(c p r) k -> c p r k", p=P, r=4)
+        rho_t = []
+        th_t = []
+
+        def load_rho(c, split):
+            t = sb.tile([P, 4, J], BF16, name="rho_raw", bufs=2, align_bytes=64)
+            if split:
+                nc.sync.dma_start(out=t[:, 0:2, :], in_=rho_v[c][:, 0:2, :])
+                nc.sync.dma_start(out=t[:, 2:4, :], in_=rho_v[c][:, 2:4, :])
+            else:
+                nc.sync.dma_start(out=t[:], in_=rho_v[c])
+            rho_t.append(t)
+
+        def load_th(c):
+            t = sb.tile([P, 4, J], U8, name="th_raw", bufs=4, align_bytes=64)
+            nc.sync.dma_start(out=t[:], in_=th_v[c])
+            th_t.append(t)
+
+        load_rho(0, True)
+        load_th(0)
+        a_raw = const.tile([P, K], I32, name="a_raw", align_bytes=64)
+        nc.sync.dma_start(out=a_raw[:], in_=a_words[0].rearrange("p n t -> p (n t)").bitcast(I32))
+        for q in range(4):
+            nc.sync.dma_start(
+                out=a_sc_raw[32 * q : 32 * q + 4, :].bitcast(I32), in_=a_scales[0, 4 * q : 4 * q + 4, :].bitcast(I32)
+            )
+        load_rho(1, False)
+        load_th(1)
+
+        gneg = const.tile([P, 8], F32, name="gneg")
+        bs = const.tile([P, 8], F32, name="bs")
+        halfpi = const.tile([P, 1], F32, name="halfpi")
+        bn = const.tile([P, 8], F32, name="bn")
+        absg = const.tile([P, 8], F32, name="absg")
+        lng = const.tile([P, 8], F32, name="lng")
+        g8 = g_t[:].rearrange("p h t -> p (h t)")
+        d8 = d1_t[:].rearrange("p h t -> p (h t)")
+        nc.vector.tensor_scalar(out=gneg[:], in0=g8, scalar1=0.0, scalar2=PI, op0=ALU.is_lt, op1=ALU.mult)
+        nc.vector.tensor_tensor(out=bs[:], in0=gneg[:], in1=d8, op=ALU.add)
+        zero = const.tile([P, 1], F32, name="zero")
+        nc.vector.memset(zero[:], 0.0)
+        nc.vector.tensor_scalar(out=halfpi[:], in0=zero[:], scalar1=PI / 2, scalar2=None, op0=ALU.add)
+        nc.vector.tensor_scalar(out=bn[:], in0=bs[:], scalar1=0.5 / PI, scalar2=None, op0=ALU.mult)
+        nc.scalar.activation(out=absg[:], in_=g8, func=ACT.Abs)
+        nc.vector.tensor_scalar(out=absg[:], in0=absg[:], scalar1=2.0**-64, scalar2=None, op0=ALU.max)
+        nc.scalar.activation(out=lng[:], in_=absg[:], func=ACT.Ln)
+
+        a_codes = const.tile([P, K], I32, name="a_codes", align_bytes=64)
+        a_sc = const.tile([P, K], U8, name="a_sc", align_bytes=64)
+        nc.vector.tensor_copy(
+            out=a_codes[:].rearrange("p (h t m) -> p h t m", h=2, t=4),
+            in_=a_raw[:].rearrange("p (h m t) -> p h t m", h=2, t=4),
+        )
+        nc.vector.tensor_copy(
+            out=a_sc[:].rearrange("p (h t m) -> p h t m", h=2, t=4),
+            in_=a_sc_raw[:].rearrange("p (h m t) -> p h t m", h=2, t=4),
+        )
+
+        w_codes = const.tile([P, 4, M], I32, name="w_codes", align_bytes=64)
+
+        def load_w():
+            for i, w in enumerate((wr_words, wp_words)):
+                for h in range(2):
+                    nc.sync.dma_start(
+                        out=w_codes[:, 2 * i + h, :], in_=w[h].rearrange("p n t -> p (n t)").bitcast(I32)
+                    )
+            for i, w in enumerate((wr_scales, wp_scales)):
+                for q in range(4):
+                    nc.sync.dma_start(
+                        out=w_sc[32 * q + 8 * i : 32 * q + 8 * i + 8, :].bitcast(I32),
+                        in_=w[:, 4 * q : 4 * q + 4, :].bitcast(I32),
+                    )
+
+        rho_q = [None] * NCH
+        th_q = [None] * NCH
+        e_t = [None] * NG
+        r_t = [None] * NG
+        s_t = [None] * NG
+        prod_q = [None] * NG
+
+        def to_codes(rows, name, bufs):
+            grp = sb.tile([P, CH * 4], BF16, name="grp", bufs=3, align_bytes=64)
+            words = rows.rearrange("p r k -> p (r k)").bitcast(F32).rearrange("p (r w u) -> p r u w", r=4, u=2)
+            for h in range(2):
+                xt = ps.tile([P, 2, 2, P], F32, name="xt", bufs=2)
+                for r in range(2):
+                    for u in range(2):
+                        nc.tensor.transpose(xt[:, r, u, :], words[:, 2 * h + r, u, :], ident[:])
+                nc.scalar.copy(
+                    out=grp[:, 1024 * h : 1024 * (h + 1)].bitcast(F32).rearrange("p (r n u) -> p r n u", r=2, u=2),
+                    in_=xt[:].rearrange("p r u n -> p r n u"),
+                )
+            codes = sb.tile([P, CH], U32, name=name + "_c", bufs=bufs, align_bytes=64)
+            scales = sb.tile([P, CH], U8, name=name + "_s", bufs=bufs, align_bytes=64)
+            nc.vector.quantize_mx(out=codes[:].bitcast(FP8X4), scales=scales[:], in_=grp[:])
+            return codes, scales
+
+        def prep_rho(c):
+            rho_q[c] = to_codes(rho_t[c][:], "rq", 2)
+
+        def prep_th(c):
+            thp = sb.tile([P, 4, J], BF16, name="thp", bufs=2, align_bytes=64)
+            for r in range(4):
+                nc.vector.tensor_tensor(out=thp[:, r, :], in0=th_t[c][:, r, :].bitcast(FP8), in1=tsc[:], op=ALU.mult)
+            th_q[c] = to_codes(thp[:], "tq", 3)
+
+        def stage1(psum, h, t, q):
+            cols = slice(512 * h + 128 * t, 512 * h + 128 * (t + 1))
+            nc.tensor.matmul_mx(
+                out=psum[:],
+                lhsT=a_codes[:, cols].bitcast(FP8X4),
+                lhsT_scale=a_sc[:, cols],
+                rhs=q[0][:].bitcast(FP8X4),
+                rhs_scale=q[1][:],
+                start=True,
+                stop=True,
+            )
+
+        def modulus(gi):
+            c, h = divmod(gi, 2)
+            e = sb.tile([P, 4, CH], F32, name="e", bufs=8)
+            for t in range(4):
+                q = ps.tile([P, CH], F32, name="qo", bufs=3)
+                stage1(q, h, t, rho_q[c])
+                nc.scalar.activation(
+                    out=e[:, t, :], in_=q[:], func=ACT.Exp, bias=lng[:, 4 * h + t : 4 * h + t + 1], scale=1.0
+                )
+            e_t[gi] = e
+
+        def reduce_phase(gi):
+            c, h = divmod(gi, 2)
+            r = sb.tile([P, 4, CH], F32, name="r", bufs=4)
+            for t in range(4):
+                psi = ps.tile([P, CH], F32, name="psi", bufs=3)
+                stage1(psi, h, t, th_q[c])
+                n = sb.tile([P, CH], I32, name="n", bufs=3)
+                j = 4 * h + t
+                nc.vector.tensor_scalar(
+                    out=n[:], in0=psi[:], scalar1=0.5 / PI, scalar2=bn[:, j : j + 1], op0=ALU.mult, op1=ALU.add
+                )
+                nc.vector.scalar_tensor_tensor(
+                    out=r[:, t, :], in0=n[:], scalar=-2 * PI, in1=psi[:], op0=ALU.mult, op1=ALU.add
+                )
+            r_t[gi] = r
+
+        def sines(gi):
+            h = gi % 2
+            s = sb.tile([P, 4, CH], F32, name="s", bufs=2)
+            r = r_t[gi]
+            for t in range(4):
+                j = 4 * h + t
+                nc.scalar.activation(out=s[:, t, :], in_=r[:, t, :], func=ACT.Abs, bias=bs[:, j : j + 1], scale=1.0)
+            for t in range(4):
+                j = 4 * h + t
+                nc.scalar.activation(out=r[:, t, :], in_=r[:, t, :], func=ACT.Sin, bias=bs[:, j : j + 1], scale=1.0)
+            nc.scalar.activation(out=s[:], in_=s[:], func=ACT.Sin, bias=halfpi[:], scale=-1.0)
+            s_t[gi] = s
+
+        def products(gi):
+            ev = e_t[gi][:].rearrange("p t (c i) -> p c t i", i=2)
+            res = []
+            for trig in (s_t[gi], r_t[gi]):
+                il = sb.tile([P, CH * 4], BF16, name="il", bufs=3, align_bytes=64)
+                nc.vector.tensor_tensor(
+                    out=il[:].rearrange("p (c i t) -> p c t i", i=2, t=4),
+                    in0=trig[:].rearrange("p t (c i) -> p c t i", i=2),
+                    in1=ev,
+                    op=ALU.mult,
+                )
+                res.append(il)
+            qs = []
+            for il in res:
+                codes = sb.tile([P, CH], U32, name="pc", bufs=8, align_bytes=64)
+                scales = sb.tile([P, CH], U8, name="pcs", bufs=8, align_bytes=64)
+                nc.vector.quantize_mx(out=codes[:].bitcast(FP8X4), scales=scales[:], in_=il[:])
+                qs.append((codes, scales))
+            prod_q[gi] = qs
+
+        out_v = out.rearrange("(c p r) m -> c p r m", p=P, r=4)
+
+        def outputs(c):
+            for r in range(4):
+                o = ps.tile([P, CH], F32, name="qo", bufs=3)
+                cols = slice(128 * r, 128 * (r + 1))
+                for x in range(4):
+                    i, h = divmod(x, 2)
+                    codes, scales = prod_q[2 * c + h][i]
+                    nc.tensor.matmul_mx(
+                        out=o[:],
+                        lhsT=codes[:, cols].bitcast(FP8X4),
+                        lhsT_scale=scales[:, cols],
+                        rhs=w_codes[:, x, :].bitcast(FP8X4),
+                        rhs_scale=w_sc[4 * x :, :],
+                        start=(x == 0),
+                        stop=(x == 3),
+                    )
+                ob = sb.tile([P, M], F32, name="ob", bufs=3)
+                nc.scalar.copy(out=ob[:], in_=o[:])
+                nc.sync.dma_start(out=out_v[c][:, r, :], in_=ob[:])
+
+        with tc.manual_schedule(engines={mybir.EngineType.Activation, mybir.EngineType.SP}):
+            for c in range(NCH):
+                prep_rho(c)
+                prep_th(c)
+                modulus(2 * c)
+                modulus(2 * c + 1)
+                if c < 2:
+                    reduce_phase(2 * c)
+                    if c == 0:
+                        reduce_phase(1)
+                if c + 2 < NCH:
+                    load_rho(c + 2, False)
+                    load_th(c + 2)
+                if c == 1:
+                    load_w()
+            for gi in range(NG):
+                sines(gi)
+                if gi + 3 < NG:
+                    reduce_phase(gi + 3)
+                products(gi)
+                if gi % 2 == 1:
+                    outputs(gi // 2)

@@ -18,10 +18,23 @@ ALU = mybir.AluOpType
 ACT = mybir.ActivationFunctionType
 
 P = 128
+PACK = 4
+ROWS = 4
+CHUNK = P * ROWS
+CHUNKS = B // CHUNK
+HALVES = K // (P * PACK)
+GROUPS = CHUNKS * HALVES
+UNITS = GROUPS * PACK
+COS, SIN = 0, 1
 PI = math.pi
-CH = 512
-NCH = B // CH
-NG = 2 * NCH
+LN_FLOOR = 2.0**-64
+
+VECTOR_COLS = 448
+
+THETA_WIDENED = (None, 2, 3, None)
+THETA_TURNED = (1, None, 2, 3)
+
+UNITS_BESIDE_SINES = (7, 3, 2, 2, 3, 2, 2, 0)
 
 
 def tile_eulerinteractionpolarlayer_w8_kernel(
@@ -29,245 +42,405 @@ def tile_eulerinteractionpolarlayer_w8_kernel(
 ):
     nc = tc.nc
     with ExitStack() as ctx:
-        const = ctx.enter_context(tc.tile_pool(name="const", bufs=1))
-        sb = ctx.enter_context(tc.tile_pool(name="sb", bufs=1))
-        ps = ctx.enter_context(tc.psum_pool(name="ps", bufs=1))
+        keep = ctx.enter_context(tc.tile_pool(name="keep", bufs=1))
+        sbuf = ctx.enter_context(tc.tile_pool(name="sbuf", bufs=1))
+        psum = ctx.enter_context(tc.psum_pool(name="psum", bufs=1))
+        ctx.enter_context(tc.manual_schedule())
 
-        tsc = const.tile([P, J], F32, name="tsc")
-        nc.scalar.dma_start(out=tsc[:], in_=theta_scale.rearrange("o k -> (o k)").partition_broadcast(P))
-        d1_t = const.tile([P, 2, 4], BF16, name="d1_t")
-        g_t = const.tile([P, 2, 4], BF16, name="g_t")
-        nc.scalar.dma_start(out=d1_t[:], in_=d1.rearrange("(h p t) -> p h t", p=P, t=4))
-        nc.scalar.dma_start(out=g_t[:], in_=g.rearrange("(h p t) -> p h t", p=P, t=4))
+        rho_in = rho.rearrange("(c p r) k -> c p r k", p=P, r=ROWS)
+        theta_in = theta_bytes.rearrange("(c p r) k -> c p r k", p=P, r=ROWS)
+        out_rows = out.rearrange("(c p r) m -> c p r m", p=P, r=ROWS)
+        rho_raw = [None] * CHUNKS
+        theta_raw = [None] * CHUNKS
 
-        ident = const.tile([P, P], F32, name="ident")
+        def load_theta(c):
+            theta_raw[c] = sbuf.tile([P, ROWS, J], U8, name="theta_raw", bufs=3, align_bytes=64)
+            nc.sync.dma_start(out=theta_raw[c][:], in_=theta_in[c])
+
+        def load_rho(c, parts=1):
+            rho_raw[c] = sbuf.tile([P, ROWS, J], BF16, name="rho_raw", bufs=2, align_bytes=64)
+            step = ROWS // parts
+            for r in range(0, ROWS, step):
+                nc.sync.dma_start(out=rho_raw[c][:, r : r + step, :], in_=rho_in[c][:, r : r + step, :])
+
+        scale_in = keep.tile([P, PACK], F32, name="scale_in")
+        g_in = keep.tile([P, HALVES, PACK], BF16, name="g_in")
+        d1_in = keep.tile([P, HALVES, PACK], BF16, name="d1_in")
+        nc.scalar.dma_start(out=scale_in[:], in_=theta_scale.rearrange("o (p t) -> p (o t)", t=PACK))
+        nc.scalar.dma_start(out=g_in[:], in_=g.rearrange("(h p t) -> p h t", p=P, t=PACK))
+        nc.scalar.dma_start(out=d1_in[:], in_=d1.rearrange("(h p t) -> p h t", p=P, t=PACK))
+        load_theta(0)
+        load_rho(0, parts=2)
+
+        ident = keep.tile([P, P], F32, name="ident")
         make_identity(nc, ident[:])
 
-        a_sc_raw = const.tile([P, K], U8, name="a_sc_raw", align_bytes=64)
-        w_sc = const.tile([P, M], U8, name="w_sc", align_bytes=64)
-        nc.vector.memset(a_sc_raw[:].bitcast(I32), 0)
-        nc.vector.memset(w_sc[:].bitcast(I32), 0)
-
-        rho_v = rho.rearrange("(c p r) k -> c p r k", p=P, r=4)
-        th_v = theta_bytes.rearrange("(c p r) k -> c p r k", p=P, r=4)
-        rho_t = []
-        th_t = []
-
-        def load_rho(c, split):
-            t = sb.tile([P, 4, J], BF16, name="rho_raw", bufs=2, align_bytes=64)
-            if split:
-                nc.sync.dma_start(out=t[:, 0:2, :], in_=rho_v[c][:, 0:2, :])
-                nc.sync.dma_start(out=t[:, 2:4, :], in_=rho_v[c][:, 2:4, :])
-            else:
-                nc.sync.dma_start(out=t[:], in_=rho_v[c])
-            rho_t.append(t)
-
-        def load_th(c):
-            t = sb.tile([P, 4, J], U8, name="th_raw", bufs=4, align_bytes=64)
-            nc.sync.dma_start(out=t[:], in_=th_v[c])
-            th_t.append(t)
-
-        load_rho(0, True)
-        load_th(0)
-        a_raw = const.tile([P, K], I32, name="a_raw", align_bytes=64)
-        nc.sync.dma_start(out=a_raw[:], in_=a_words[0].rearrange("p n t -> p (n t)").bitcast(I32))
+        zero = keep.tile([P, 1], F32, name="zero")
+        a_scales_raw = keep.tile([P, K], U8, name="a_scales_raw", align_bytes=64)
+        w_scales = keep.tile([P, M], U8, name="w_scales", align_bytes=64)
+        nc.vector.memset(zero[:], 0.0)
+        nc.vector.memset(a_scales_raw[:].bitcast(I32), 0)
+        nc.vector.memset(w_scales[:].bitcast(I32), 0)
+        a_codes_raw = keep.tile([P, K], I32, name="a_codes_raw", align_bytes=64)
+        nc.sync.dma_start(out=a_codes_raw[:], in_=a_words[0].rearrange("p n t -> p (n t)").bitcast(I32))
         for q in range(4):
             nc.sync.dma_start(
-                out=a_sc_raw[32 * q : 32 * q + 4, :].bitcast(I32), in_=a_scales[0, 4 * q : 4 * q + 4, :].bitcast(I32)
+                out=a_scales_raw[32 * q : 32 * q + 4, :].bitcast(I32),
+                in_=a_scales[0, 4 * q : 4 * q + 4, :].bitcast(I32),
             )
-        load_rho(1, False)
-        load_th(1)
 
-        gneg = const.tile([P, 8], F32, name="gneg")
-        bs = const.tile([P, 8], F32, name="bs")
-        halfpi = const.tile([P, 1], F32, name="halfpi")
-        bn = const.tile([P, 8], F32, name="bn")
-        absg = const.tile([P, 8], F32, name="absg")
-        lng = const.tile([P, 8], F32, name="lng")
-        g8 = g_t[:].rearrange("p h t -> p (h t)")
-        d8 = d1_t[:].rearrange("p h t -> p (h t)")
-        nc.vector.tensor_scalar(out=gneg[:], in0=g8, scalar1=0.0, scalar2=PI, op0=ALU.is_lt, op1=ALU.mult)
-        nc.vector.tensor_tensor(out=bs[:], in0=gneg[:], in1=d8, op=ALU.add)
-        zero = const.tile([P, 1], F32, name="zero")
-        nc.vector.memset(zero[:], 0.0)
-        nc.vector.tensor_scalar(out=halfpi[:], in0=zero[:], scalar1=PI / 2, scalar2=None, op0=ALU.add)
-        nc.vector.tensor_scalar(out=bn[:], in0=bs[:], scalar1=0.5 / PI, scalar2=None, op0=ALU.mult)
-        nc.scalar.activation(out=absg[:], in_=g8, func=ACT.Abs)
-        nc.vector.tensor_scalar(out=absg[:], in0=absg[:], scalar1=2.0**-64, scalar2=None, op0=ALU.max)
-        nc.scalar.activation(out=lng[:], in_=absg[:], func=ACT.Ln)
+        w_codes = keep.tile([P, 2 * HALVES, M], I32, name="w_codes", align_bytes=64)
 
-        a_codes = const.tile([P, K], I32, name="a_codes", align_bytes=64)
-        a_sc = const.tile([P, K], U8, name="a_sc", align_bytes=64)
-        nc.vector.tensor_copy(
-            out=a_codes[:].rearrange("p (h t m) -> p h t m", h=2, t=4),
-            in_=a_raw[:].rearrange("p (h m t) -> p h t m", h=2, t=4),
-        )
-        nc.vector.tensor_copy(
-            out=a_sc[:].rearrange("p (h t m) -> p h t m", h=2, t=4),
-            in_=a_sc_raw[:].rearrange("p (h m t) -> p h t m", h=2, t=4),
-        )
-
-        w_codes = const.tile([P, 4, M], I32, name="w_codes", align_bytes=64)
-
-        def load_w():
-            for i, w in enumerate((wr_words, wp_words)):
-                for h in range(2):
+        def load_output_weights():
+            for w, words in ((COS, wr_words), (SIN, wp_words)):
+                for h in range(HALVES):
                     nc.sync.dma_start(
-                        out=w_codes[:, 2 * i + h, :], in_=w[h].rearrange("p n t -> p (n t)").bitcast(I32)
+                        out=w_codes[:, HALVES * w + h, :], in_=words[h].rearrange("p n t -> p (n t)").bitcast(I32)
                     )
-            for i, w in enumerate((wr_scales, wp_scales)):
+            for w, scales in ((COS, wr_scales), (SIN, wp_scales)):
                 for q in range(4):
+                    first = 32 * q + 8 * w
                     nc.sync.dma_start(
-                        out=w_sc[32 * q + 8 * i : 32 * q + 8 * i + 8, :].bitcast(I32),
-                        in_=w[:, 4 * q : 4 * q + 4, :].bitcast(I32),
+                        out=w_scales[first : first + 8, :].bitcast(I32),
+                        in_=scales[:, 4 * q : 4 * q + 4, :].bitcast(I32),
                     )
 
-        rho_q = [None] * NCH
-        th_q = [None] * NCH
-        e_t = [None] * NG
-        r_t = [None] * NG
-        s_t = [None] * NG
-        prod_q = [None] * NG
+        abs_g = keep.tile([P, HALVES * PACK], F32, name="abs_g")
+        ln_g = keep.tile([P, HALVES * PACK], F32, name="ln_g")
+        sign_phase = keep.tile([P, HALVES * PACK], F32, name="sign_phase")
+        phase = keep.tile([P, HALVES * PACK], F32, name="phase")
+        phase_turns = keep.tile([P, HALVES * PACK], F32, name="phase_turns")
+        half_pi = keep.tile([P, 1], F32, name="half_pi")
+        g_flat = g_in[:].rearrange("p h t -> p (h t)")
+        d1_flat = d1_in[:].rearrange("p h t -> p (h t)")
+        nc.vector.scalar_tensor_tensor(out=abs_g[:], in0=g_flat, scalar=-1.0, in1=g_flat, op0=ALU.mult, op1=ALU.max)
+        nc.vector.tensor_scalar(out=half_pi[:], in0=zero[:], scalar1=PI / 2, scalar2=None, op0=ALU.add)
+        nc.vector.tensor_scalar(
+            out=sign_phase[:], in0=g_flat, scalar1=0.0, scalar2=PI, op0=ALU.is_lt, op1=ALU.mult
+        )
+        nc.vector.tensor_scalar(out=abs_g[:], in0=abs_g[:], scalar1=LN_FLOOR, scalar2=None, op0=ALU.max)
+        nc.vector.tensor_tensor(out=phase[:], in0=sign_phase[:], in1=d1_flat, op=ALU.add)
+        nc.vector.tensor_scalar(out=phase_turns[:], in0=phase[:], scalar1=0.5 / PI, scalar2=None, op0=ALU.mult)
+        nc.scalar.activation(out=ln_g[:], in_=abs_g[:], func=ACT.Ln)
 
-        def to_codes(rows, name, bufs):
-            grp = sb.tile([P, CH * 4], BF16, name="grp", bufs=3, align_bytes=64)
-            words = rows.rearrange("p r k -> p (r k)").bitcast(F32).rearrange("p (r w u) -> p r u w", r=4, u=2)
-            for h in range(2):
-                xt = ps.tile([P, 2, 2, P], F32, name="xt", bufs=2)
-                for r in range(2):
-                    for u in range(2):
-                        nc.tensor.transpose(xt[:, r, u, :], words[:, 2 * h + r, u, :], ident[:])
-                nc.scalar.copy(
-                    out=grp[:, 1024 * h : 1024 * (h + 1)].bitcast(F32).rearrange("p (r n u) -> p r n u", r=2, u=2),
-                    in_=xt[:].rearrange("p r u n -> p r n u"),
+        theta_scales = keep.tile([P, J], F32, name="theta_scales")
+
+        def spread_theta_scales():
+            bank = psum.tile([P, PACK, P], F32, name="turn", bufs=2)
+            for t in range(PACK):
+                nc.tensor.transpose(bank[:, t, :], scale_in[:, t : t + 1].to_broadcast([P, P]), ident[:])
+            nc.scalar.copy(
+                out=theta_scales[:].rearrange("p (n t) -> p n t", t=PACK), in_=bank[:].rearrange("p t n -> p n t")
+            )
+
+        a_codes = keep.tile([P, K], I32, name="a_codes", align_bytes=64)
+        a_scale_plane = keep.tile([P, K], U8, name="a_scale_plane", align_bytes=64)
+
+        def reorder_a():
+            for to, source in ((a_codes, a_codes_raw), (a_scale_plane, a_scales_raw)):
+                nc.vector.tensor_copy(
+                    out=to[:].rearrange("p (h t m) -> p h t m", h=HALVES, t=PACK),
+                    in_=source[:].rearrange("p (h m t) -> p h t m", h=HALVES, t=PACK),
                 )
-            codes = sb.tile([P, CH], U32, name=name + "_c", bufs=bufs, align_bytes=64)
-            scales = sb.tile([P, CH], U8, name=name + "_s", bufs=bufs, align_bytes=64)
-            nc.vector.quantize_mx(out=codes[:].bitcast(FP8X4), scales=scales[:], in_=grp[:])
+
+        rho_packed = [None] * CHUNKS
+        rho_codes = [None] * CHUNKS
+        theta_wide = [None] * CHUNKS
+        theta_packed = [None] * CHUNKS
+        theta_codes = [None] * CHUNKS
+
+        def widen_theta(c, r):
+            if r == 0:
+                theta_wide[c] = sbuf.tile([P, ROWS, J], BF16, name="theta_wide", bufs=2, align_bytes=64)
+            nc.vector.tensor_tensor(
+                out=theta_wide[c][:, r, :],
+                in0=theta_raw[c][:, r, :].bitcast(FP8),
+                in1=theta_scales[:],
+                op=ALU.mult,
+            )
+
+        def turn(source, packed):
+            words = source[:].rearrange("p r k -> p (r k)").bitcast(F32).rearrange("p (r w u) -> p r u w", r=ROWS, u=2)
+            packed_words = packed[:].bitcast(F32).rearrange("p (r n u) -> p r n u", r=ROWS, u=2)
+            for r in range(0, ROWS, 2):
+                bank = psum.tile([P, 2, 2, P], F32, name="turn", bufs=2)
+                for i in range(2):
+                    for u in range(2):
+                        nc.tensor.transpose(bank[:, i, u, :], words[:, r + i, u, :], ident[:])
+                nc.scalar.copy(out=packed_words[:, r : r + 2, :, :], in_=bank[:].rearrange("p r u n -> p r n u"))
+
+        def turn_rho(c):
+            rho_packed[c] = sbuf.tile([P, CHUNK * PACK], BF16, name="packed", bufs=3, align_bytes=64)
+            turn(rho_raw[c], rho_packed[c])
+
+        def turn_theta(c):
+            theta_packed[c] = sbuf.tile([P, CHUNK * PACK], BF16, name="packed", bufs=3, align_bytes=64)
+            turn(theta_wide[c], theta_packed[c])
+
+        def quantise(packed, name, bufs):
+            codes = sbuf.tile([P, CHUNK], U32, name=name + "_codes", bufs=bufs, align_bytes=64)
+            scales = sbuf.tile([P, CHUNK], U8, name=name + "_scales", bufs=bufs, align_bytes=64)
+            nc.vector.quantize_mx(out=codes[:].bitcast(FP8X4), scales=scales[:], in_=packed[:])
             return codes, scales
 
-        def prep_rho(c):
-            rho_q[c] = to_codes(rho_t[c][:], "rq", 2)
+        def quantise_rho(c):
+            rho_codes[c] = quantise(rho_packed[c], "rho", 2)
 
-        def prep_th(c):
-            thp = sb.tile([P, 4, J], BF16, name="thp", bufs=2, align_bytes=64)
-            for r in range(4):
-                nc.vector.tensor_tensor(out=thp[:, r, :], in0=th_t[c][:, r, :].bitcast(FP8), in1=tsc[:], op=ALU.mult)
-            th_q[c] = to_codes(thp[:], "tq", 3)
+        def quantise_theta(c):
+            theta_codes[c] = quantise(theta_packed[c], "theta", CHUNKS)
 
-        def stage1(psum, h, t, q):
-            cols = slice(512 * h + 128 * t, 512 * h + 128 * (t + 1))
+        def unit(u):
+            group, t = divmod(u, PACK)
+            c, h = divmod(group, HALVES)
+            return group, c, h, t
+
+        def channel_column(u):
+            return slice(u % (HALVES * PACK), u % (HALVES * PACK) + 1)
+
+        def first_product(bank, h, t, codes, scales):
+            cols = slice(P * (PACK * h + t), P * (PACK * h + t + 1))
             nc.tensor.matmul_mx(
-                out=psum[:],
+                out=bank[:],
                 lhsT=a_codes[:, cols].bitcast(FP8X4),
-                lhsT_scale=a_sc[:, cols],
-                rhs=q[0][:].bitcast(FP8X4),
-                rhs_scale=q[1][:],
+                lhsT_scale=a_scale_plane[:, cols],
+                rhs=codes[:].bitcast(FP8X4),
+                rhs_scale=scales[:],
                 start=True,
                 stop=True,
             )
 
-        def modulus(gi):
-            c, h = divmod(gi, 2)
-            e = sb.tile([P, 4, CH], F32, name="e", bufs=8)
-            for t in range(4):
-                q = ps.tile([P, CH], F32, name="qo", bufs=3)
-                stage1(q, h, t, rho_q[c])
+        modulus = [None] * GROUPS
+
+        def exponential(u):
+            group, c, h, t = unit(u)
+            if t == 0:
+                modulus[group] = sbuf.tile([P, PACK, CHUNK], F32, name="modulus", bufs=GROUPS)
+            q = psum.tile([P, CHUNK], F32, name="bank", bufs=3)
+            first_product(q, h, t, *rho_codes[c])
+            nc.scalar.activation(
+                out=modulus[group][:, t, :], in_=q[:], func=ACT.Exp, bias=ln_g[:, channel_column(u)], scale=1.0
+            )
+
+        psi_bank = [None] * UNITS
+        turns = [None] * UNITS
+        angle = [None] * GROUPS
+        cosine = [None] * GROUPS
+
+        def psi_product(u):
+            group, c, h, t = unit(u)
+            psi_bank[u] = psum.tile([P, CHUNK], F32, name="psi", bufs=3)
+            first_product(psi_bank[u], h, t, *theta_codes[c])
+
+        def count_turns(u):
+            turns[u] = sbuf.tile([P, CHUNK], I32, name="turns", bufs=3)
+            nc.vector.tensor_scalar(
+                out=turns[u][:],
+                in0=psi_bank[u][:],
+                scalar1=0.5 / PI,
+                scalar2=phase_turns[:, channel_column(u)],
+                op0=ALU.mult,
+                op1=ALU.add,
+            )
+
+        def take_turns_off(u):
+            group, c, h, t = unit(u)
+            if t == 0:
+                angle[group] = sbuf.tile([P, PACK, CHUNK], F32, name="angle", bufs=5)
+            nc.vector.scalar_tensor_tensor(
+                out=angle[group][:, t, :],
+                in0=turns[u][:],
+                scalar=-2 * PI,
+                in1=psi_bank[u][:],
+                op0=ALU.mult,
+                op1=ALU.add,
+            )
+
+        def phase_step(u):
+            if u == 0:
+                psi_product(0)
+            if u + 1 < UNITS:
+                psi_product(u + 1)
+            if u < UNITS:
+                count_turns(u)
+            if u > 0:
+                take_turns_off(u - 1)
+
+        def with_phase(target, group, func):
+            for t in range(PACK):
                 nc.scalar.activation(
-                    out=e[:, t, :], in_=q[:], func=ACT.Exp, bias=lng[:, 4 * h + t : 4 * h + t + 1], scale=1.0
+                    out=target[:, t, :],
+                    in_=angle[group][:, t, :],
+                    func=func,
+                    bias=phase[:, channel_column(PACK * group + t)],
+                    scale=1.0,
                 )
-            e_t[gi] = e
 
-        def reduce_phase(gi):
-            c, h = divmod(gi, 2)
-            r = sb.tile([P, 4, CH], F32, name="r", bufs=4)
-            for t in range(4):
-                psi = ps.tile([P, CH], F32, name="psi", bufs=3)
-                stage1(psi, h, t, th_q[c])
-                n = sb.tile([P, CH], I32, name="n", bufs=3)
-                j = 4 * h + t
-                nc.vector.tensor_scalar(
-                    out=n[:], in0=psi[:], scalar1=0.5 / PI, scalar2=bn[:, j : j + 1], op0=ALU.mult, op1=ALU.add
+        def absolute(group):
+            cosine[group] = sbuf.tile([P, PACK, CHUNK], F32, name="cosine", bufs=2)
+            with_phase(cosine[group], group, ACT.Abs)
+
+        def sine(group):
+            with_phase(angle[group], group, ACT.Sin)
+
+        def cosine_of_absolute(group, first=0, end=CHUNK):
+            part = cosine[group][:, :, first:end]
+            nc.scalar.activation(out=part, in_=part, func=ACT.Sin, bias=half_pi[:], scale=-1.0)
+
+        product_packed = {}
+        product_codes = {}
+
+        def multiply(engine, group, w, first=0, end=CHUNK):
+            if first == 0:
+                product_packed[group, w] = sbuf.tile([P, CHUNK * PACK], BF16, name="packed_product", bufs=3, align_bytes=64)
+            trig = (cosine, angle)[w][group]
+            engine.tensor_tensor(
+                out=product_packed[group, w][:, PACK * first : PACK * end].rearrange(
+                    "p (c i t) -> p c t i", i=2, t=PACK
+                ),
+                in0=trig[:, :, first:end].rearrange("p t (c i) -> p c t i", i=2),
+                in1=modulus[group][:, :, first:end].rearrange("p t (c i) -> p c t i", i=2),
+                op=ALU.mult,
+            )
+
+        def multiply_shared(group, w):
+            multiply(nc.vector, group, w, 0, VECTOR_COLS)
+            multiply(nc.gpsimd, group, w, VECTOR_COLS, CHUNK)
+
+        def quantise_product(group, w, first=0, end=CHUNK):
+            if first == 0:
+                product_codes[group, w] = (
+                    sbuf.tile([P, CHUNK], U32, name="product_codes", bufs=6, align_bytes=64),
+                    sbuf.tile([P, CHUNK], U8, name="product_scales", bufs=6, align_bytes=64),
                 )
-                nc.vector.scalar_tensor_tensor(
-                    out=r[:, t, :], in0=n[:], scalar=-2 * PI, in1=psi[:], op0=ALU.mult, op1=ALU.add
+            codes, scales = product_codes[group, w]
+            nc.vector.quantize_mx(
+                out=codes[:, first:end].bitcast(FP8X4),
+                scales=scales[:, first:end],
+                in_=product_packed[group, w][:, PACK * first : PACK * end],
+            )
+
+        passes = ((0, SIN), (0, COS), (1, SIN), (1, COS))
+
+        def output_passes(bank, c, r, which):
+            cols = slice(P * r, P * (r + 1))
+            for i in which:
+                h, w = passes[i]
+                codes, scales = product_codes[HALVES * c + h, w]
+                plane = HALVES * w + h
+                nc.tensor.matmul_mx(
+                    out=bank[:],
+                    lhsT=codes[:, cols].bitcast(FP8X4),
+                    lhsT_scale=scales[:, cols],
+                    rhs=w_codes[:, plane, :].bitcast(FP8X4),
+                    rhs_scale=w_scales[4 * plane :, :],
+                    start=(i == 0),
+                    stop=(i == len(passes) - 1),
                 )
-            r_t[gi] = r
 
-        def sines(gi):
-            h = gi % 2
-            s = sb.tile([P, 4, CH], F32, name="s", bufs=2)
-            r = r_t[gi]
-            for t in range(4):
-                j = 4 * h + t
-                nc.scalar.activation(out=s[:, t, :], in_=r[:, t, :], func=ACT.Abs, bias=bs[:, j : j + 1], scale=1.0)
-            for t in range(4):
-                j = 4 * h + t
-                nc.scalar.activation(out=r[:, t, :], in_=r[:, t, :], func=ACT.Sin, bias=bs[:, j : j + 1], scale=1.0)
-            nc.scalar.activation(out=s[:], in_=s[:], func=ACT.Sin, bias=halfpi[:], scale=-1.0)
-            s_t[gi] = s
+        def store_output(bank, c, r, copy):
+            rows = sbuf.tile([P, M], F32, name="out_rows", bufs=6)
+            copy(out=rows[:], in_=bank[:])
+            nc.sync.dma_start(out=out_rows[c][:, r, :], in_=rows[:])
 
-        def products(gi):
-            ev = e_t[gi][:].rearrange("p t (c i) -> p c t i", i=2)
-            res = []
-            for trig in (s_t[gi], r_t[gi]):
-                il = sb.tile([P, CH * 4], BF16, name="il", bufs=3, align_bytes=64)
-                nc.vector.tensor_tensor(
-                    out=il[:].rearrange("p (c i t) -> p c t i", i=2, t=4),
-                    in0=trig[:].rearrange("p t (c i) -> p c t i", i=2),
-                    in1=ev,
-                    op=ALU.mult,
-                )
-                res.append(il)
-            qs = []
-            for il in res:
-                codes = sb.tile([P, CH], U32, name="pc", bufs=8, align_bytes=64)
-                scales = sb.tile([P, CH], U8, name="pcs", bufs=8, align_bytes=64)
-                nc.vector.quantize_mx(out=codes[:].bitcast(FP8X4), scales=scales[:], in_=il[:])
-                qs.append((codes, scales))
-            prod_q[gi] = qs
+        def output_bank(r, idle_ring, idle_bufs):
+            if r < ROWS - 1:
+                bank = psum.tile([P, M], F32, name="bank", bufs=3)
+            else:
+                bank = psum.tile([P, M], F32, name=idle_ring, bufs=idle_bufs)
+            return bank
 
-        out_v = out.rearrange("(c p r) m -> c p r m", p=P, r=4)
+        spread_theta_scales()
+        turn_rho(0)
+        for r in range(ROWS):
+            widen_theta(0, r)
+        turn_theta(0)
+        reorder_a()
+        quantise_rho(0)
+        load_rho(1)
+        load_theta(1)
+        load_theta(2)
+        for r in range(ROWS):
+            widen_theta(1, r)
+        quantise_theta(0)
 
-        def outputs(c):
-            for r in range(4):
-                o = ps.tile([P, CH], F32, name="qo", bufs=3)
-                cols = slice(128 * r, 128 * (r + 1))
-                for x in range(4):
-                    i, h = divmod(x, 2)
-                    codes, scales = prod_q[2 * c + h][i]
-                    nc.tensor.matmul_mx(
-                        out=o[:],
-                        lhsT=codes[:, cols].bitcast(FP8X4),
-                        lhsT_scale=scales[:, cols],
-                        rhs=w_codes[:, x, :].bitcast(FP8X4),
-                        rhs_scale=w_sc[4 * x :, :],
-                        start=(x == 0),
-                        stop=(x == 3),
-                    )
-                ob = sb.tile([P, M], F32, name="ob", bufs=3)
-                nc.scalar.copy(out=ob[:], in_=o[:])
-                nc.sync.dma_start(out=out_v[c][:, r, :], in_=ob[:])
+        for c in range(CHUNKS):
+            for k in range(4):
+                exponential(8 * c + 2 * k)
+                exponential(8 * c + 2 * k + 1)
+                if k == 0:
+                    if c + 1 < CHUNKS:
+                        turn_rho(c + 1)
+                    continue
+                if k == 1 and c > 0 and THETA_TURNED[c - 1] is not None:
+                    quantise_theta(THETA_TURNED[c - 1])
+                if k == 2 and THETA_TURNED[c] is not None:
+                    turn_theta(THETA_TURNED[c])
+                phase_step(3 * c + k - 1)
+                if k == 2:
+                    if c + 1 < CHUNKS:
+                        quantise_rho(c + 1)
+                    if c + 2 < CHUNKS:
+                        load_rho(c + 2)
+                elif THETA_WIDENED[c] is not None:
+                    widen_theta(THETA_WIDENED[c], k - 1)
+                    widen_theta(THETA_WIDENED[c], k)
+                if c == 0 and k == 1:
+                    load_output_weights()
+                if c == 0 and k == 3:
+                    load_theta(3)
 
-        with tc.manual_schedule(engines={mybir.EngineType.Activation, mybir.EngineType.SP}):
-            for c in range(NCH):
-                prep_rho(c)
-                prep_th(c)
-                modulus(2 * c)
-                modulus(2 * c + 1)
-                if c < 2:
-                    reduce_phase(2 * c)
-                    if c == 0:
-                        reduce_phase(1)
-                if c + 2 < NCH:
-                    load_rho(c + 2, False)
-                    load_th(c + 2)
-                if c == 1:
-                    load_w()
-            for gi in range(NG):
-                sines(gi)
-                if gi + 3 < NG:
-                    reduce_phase(gi + 3)
-                products(gi)
-                if gi % 2 == 1:
-                    outputs(gi // 2)
+        next_unit = 3 * CHUNKS
+        for group in range(GROUPS):
+            count = UNITS_BESIDE_SINES[group]
+            units = list(range(next_unit, next_unit + count))
+            next_unit += count
+            c = (group - 3) // 2 if group >= 3 and group % 2 == 1 else None
+            banks = []
+            if group == 0:
+                for u in units:
+                    phase_step(u)
+                quantise_theta(CHUNKS - 1)
+            else:
+                half = (count + 1) // 2
+                for w, share, rows in ((SIN, units[:half], (0, 1)), (COS, units[half:], (2, 3))):
+                    multiply_shared(group - 1, w)
+                    for u in share[:1]:
+                        phase_step(u)
+                    if c is not None:
+                        for r in rows:
+                            banks.append(output_bank(r, "turn", 2))
+                            output_passes(banks[r], c, r, range(4))
+                    for u in share[1:]:
+                        phase_step(u)
+                quantise_product(group - 1, SIN)
+                quantise_product(group - 1, COS)
+
+            absolute(group)
+            if c is not None:
+                store_output(banks[0], c, 0, nc.scalar.copy)
+            sine(group)
+            if c is not None:
+                store_output(banks[1], c, 1, nc.scalar.copy)
+                store_output(banks[2], c, 2, nc.scalar.copy)
+            quarters = 1 if group < GROUPS - 1 else 4
+            for i in range(quarters):
+                cosine_of_absolute(group, i * CHUNK // quarters, (i + 1) * CHUNK // quarters)
+            if c is not None:
+                store_output(banks[3], c, 3, nc.scalar.copy)
+
+        group = GROUPS - 1
+        c = CHUNKS - 1
+        multiply(nc.vector, group, SIN)
+        quantise_product(group, SIN)
+        for r in range(ROWS + 1):
+            if r < ROWS:
+                multiply(nc.vector, group, COS, P * r, P * (r + 1))
+            if r > 0:
+                quantise_product(group, COS, P * (r - 1), P * r)
+        banks = [output_bank(r, "psi", 3) for r in range(ROWS)]
+        for which in ((0, 1), (2,)):
+            for r in range(ROWS):
+                output_passes(banks[r], c, r, which)
+        for r in range(ROWS):
+            output_passes(banks[r], c, r, (3,))
+            store_output(banks[r], c, r, (nc.scalar.copy, nc.vector.tensor_copy)[r % 2])

import math
from contextlib import ExitStack

import concourse.mybir as mybir
from concourse.masks import make_identity

B, J, K, M = 2048, 512, 1024, 512
FLOPS = 2 * 2 * B * J * K + 2 * 2 * B * K * M

F32 = mybir.dt.float32
BF16 = mybir.dt.bfloat16
FP8 = mybir.dt.float8_e4m3fn
FP8X4 = mybir.dt.float8_e4m3fn_x4
I32 = mybir.dt.int32
U32 = mybir.dt.uint32
U8 = mybir.dt.uint8
ALU = mybir.AluOpType
ACT = mybir.ActivationFunctionType

P = 128
PACK = 4
ROWS = 4
CHUNK = P * ROWS
CHUNKS = B // CHUNK
HALVES = K // (P * PACK)
GROUPS = CHUNKS * HALVES
UNITS = GROUPS * PACK
COS, SIN = 0, 1
PI = math.pi
LN_FLOOR = 2.0**-64

VECTOR_COLS = 448

THETA_WIDENED = (None, 2, 3, None)
THETA_TURNED = (1, None, 2, 3)

UNITS_BESIDE_SINES = (7, 3, 2, 2, 3, 2, 2, 0)


def tile_eulerinteractionpolarlayer_w8_kernel(
    tc, theta_bytes, theta_scale, rho, a_words, a_scales, d1, g, wr_words, wr_scales, wp_words, wp_scales, out
):
    nc = tc.nc
    with ExitStack() as ctx:
        keep = ctx.enter_context(tc.tile_pool(name="keep", bufs=1))
        sbuf = ctx.enter_context(tc.tile_pool(name="sbuf", bufs=1))
        psum = ctx.enter_context(tc.psum_pool(name="psum", bufs=1))
        ctx.enter_context(tc.manual_schedule())

        rho_in = rho.rearrange("(c p r) k -> c p r k", p=P, r=ROWS)
        theta_in = theta_bytes.rearrange("(c p r) k -> c p r k", p=P, r=ROWS)
        out_rows = out.rearrange("(c p r) m -> c p r m", p=P, r=ROWS)
        rho_raw = [None] * CHUNKS
        theta_raw = [None] * CHUNKS

        def load_theta(c):
            theta_raw[c] = sbuf.tile([P, ROWS, J], U8, name="theta_raw", bufs=3, align_bytes=64)
            nc.sync.dma_start(out=theta_raw[c][:], in_=theta_in[c])

        def load_rho(c, parts=1):
            rho_raw[c] = sbuf.tile([P, ROWS, J], BF16, name="rho_raw", bufs=2, align_bytes=64)
            step = ROWS // parts
            for r in range(0, ROWS, step):
                nc.sync.dma_start(out=rho_raw[c][:, r : r + step, :], in_=rho_in[c][:, r : r + step, :])

        scale_in = keep.tile([P, PACK], F32, name="scale_in")
        g_in = keep.tile([P, HALVES, PACK], BF16, name="g_in")
        d1_in = keep.tile([P, HALVES, PACK], BF16, name="d1_in")
        nc.scalar.dma_start(out=scale_in[:], in_=theta_scale.rearrange("o (p t) -> p (o t)", t=PACK))
        nc.scalar.dma_start(out=g_in[:], in_=g.rearrange("(h p t) -> p h t", p=P, t=PACK))
        nc.scalar.dma_start(out=d1_in[:], in_=d1.rearrange("(h p t) -> p h t", p=P, t=PACK))
        load_theta(0)
        load_rho(0, parts=2)

        ident = keep.tile([P, P], F32, name="ident")
        make_identity(nc, ident[:])

        zero = keep.tile([P, 1], F32, name="zero")
        a_scales_raw = keep.tile([P, K], U8, name="a_scales_raw", align_bytes=64)
        w_scales = keep.tile([P, M], U8, name="w_scales", align_bytes=64)
        nc.vector.memset(zero[:], 0.0)
        nc.vector.memset(a_scales_raw[:].bitcast(I32), 0)
        nc.vector.memset(w_scales[:].bitcast(I32), 0)
        a_codes_raw = keep.tile([P, K], I32, name="a_codes_raw", align_bytes=64)
        nc.sync.dma_start(out=a_codes_raw[:], in_=a_words[0].rearrange("p n t -> p (n t)").bitcast(I32))
        for q in range(4):
            nc.sync.dma_start(
                out=a_scales_raw[32 * q : 32 * q + 4, :].bitcast(I32),
                in_=a_scales[0, 4 * q : 4 * q + 4, :].bitcast(I32),
            )

        w_codes = keep.tile([P, 2 * HALVES, M], I32, name="w_codes", align_bytes=64)

        def load_output_weights():
            for w, words in ((COS, wr_words), (SIN, wp_words)):
                for h in range(HALVES):
                    nc.sync.dma_start(
                        out=w_codes[:, HALVES * w + h, :], in_=words[h].rearrange("p n t -> p (n t)").bitcast(I32)
                    )
            for w, scales in ((COS, wr_scales), (SIN, wp_scales)):
                for q in range(4):
                    first = 32 * q + 8 * w
                    nc.sync.dma_start(
                        out=w_scales[first : first + 8, :].bitcast(I32),
                        in_=scales[:, 4 * q : 4 * q + 4, :].bitcast(I32),
                    )

        abs_g = keep.tile([P, HALVES * PACK], F32, name="abs_g")
        ln_g = keep.tile([P, HALVES * PACK], F32, name="ln_g")
        sign_phase = keep.tile([P, HALVES * PACK], F32, name="sign_phase")
        phase = keep.tile([P, HALVES * PACK], F32, name="phase")
        phase_turns = keep.tile([P, HALVES * PACK], F32, name="phase_turns")
        half_pi = keep.tile([P, 1], F32, name="half_pi")
        g_flat = g_in[:].rearrange("p h t -> p (h t)")
        d1_flat = d1_in[:].rearrange("p h t -> p (h t)")
        nc.vector.scalar_tensor_tensor(out=abs_g[:], in0=g_flat, scalar=-1.0, in1=g_flat, op0=ALU.mult, op1=ALU.max)
        nc.vector.tensor_scalar(out=half_pi[:], in0=zero[:], scalar1=PI / 2, scalar2=None, op0=ALU.add)
        nc.vector.tensor_scalar(
            out=sign_phase[:], in0=g_flat, scalar1=0.0, scalar2=PI, op0=ALU.is_lt, op1=ALU.mult
        )
        nc.vector.tensor_scalar(out=abs_g[:], in0=abs_g[:], scalar1=LN_FLOOR, scalar2=None, op0=ALU.max)
        nc.vector.tensor_tensor(out=phase[:], in0=sign_phase[:], in1=d1_flat, op=ALU.add)
        nc.vector.tensor_scalar(out=phase_turns[:], in0=phase[:], scalar1=0.5 / PI, scalar2=None, op0=ALU.mult)
        nc.scalar.activation(out=ln_g[:], in_=abs_g[:], func=ACT.Ln)

        theta_scales = keep.tile([P, J], F32, name="theta_scales")

        def spread_theta_scales():
            bank = psum.tile([P, PACK, P], F32, name="turn", bufs=2)
            for t in range(PACK):
                nc.tensor.transpose(bank[:, t, :], scale_in[:, t : t + 1].to_broadcast([P, P]), ident[:])
            nc.scalar.copy(
                out=theta_scales[:].rearrange("p (n t) -> p n t", t=PACK), in_=bank[:].rearrange("p t n -> p n t")
            )

        a_codes = keep.tile([P, K], I32, name="a_codes", align_bytes=64)
        a_scale_plane = keep.tile([P, K], U8, name="a_scale_plane", align_bytes=64)

        def reorder_a():
            for to, source in ((a_codes, a_codes_raw), (a_scale_plane, a_scales_raw)):
                nc.vector.tensor_copy(
                    out=to[:].rearrange("p (h t m) -> p h t m", h=HALVES, t=PACK),
                    in_=source[:].rearrange("p (h m t) -> p h t m", h=HALVES, t=PACK),
                )

        rho_packed = [None] * CHUNKS
        rho_codes = [None] * CHUNKS
        theta_wide = [None] * CHUNKS
        theta_packed = [None] * CHUNKS
        theta_codes = [None] * CHUNKS

        def widen_theta(c, r):
            if r == 0:
                theta_wide[c] = sbuf.tile([P, ROWS, J], BF16, name="theta_wide", bufs=2, align_bytes=64)
            nc.vector.tensor_tensor(
                out=theta_wide[c][:, r, :],
                in0=theta_raw[c][:, r, :].bitcast(FP8),
                in1=theta_scales[:],
                op=ALU.mult,
            )

        def turn(source, packed):
            words = source[:].rearrange("p r k -> p (r k)").bitcast(F32).rearrange("p (r w u) -> p r u w", r=ROWS, u=2)
            packed_words = packed[:].bitcast(F32).rearrange("p (r n u) -> p r n u", r=ROWS, u=2)
            for r in range(0, ROWS, 2):
                bank = psum.tile([P, 2, 2, P], F32, name="turn", bufs=2)
                for i in range(2):
                    for u in range(2):
                        nc.tensor.transpose(bank[:, i, u, :], words[:, r + i, u, :], ident[:])
                nc.scalar.copy(out=packed_words[:, r : r + 2, :, :], in_=bank[:].rearrange("p r u n -> p r n u"))

        def turn_rho(c):
            rho_packed[c] = sbuf.tile([P, CHUNK * PACK], BF16, name="packed", bufs=3, align_bytes=64)
            turn(rho_raw[c], rho_packed[c])

        def turn_theta(c):
            theta_packed[c] = sbuf.tile([P, CHUNK * PACK], BF16, name="packed", bufs=3, align_bytes=64)
            turn(theta_wide[c], theta_packed[c])

        def quantise(packed, name, bufs):
            codes = sbuf.tile([P, CHUNK], U32, name=name + "_codes", bufs=bufs, align_bytes=64)
            scales = sbuf.tile([P, CHUNK], U8, name=name + "_scales", bufs=bufs, align_bytes=64)
            nc.vector.quantize_mx(out=codes[:].bitcast(FP8X4), scales=scales[:], in_=packed[:])
            return codes, scales

        def quantise_rho(c):
            rho_codes[c] = quantise(rho_packed[c], "rho", 2)

        def quantise_theta(c):
            theta_codes[c] = quantise(theta_packed[c], "theta", CHUNKS)

        def unit(u):
            group, t = divmod(u, PACK)
            c, h = divmod(group, HALVES)
            return group, c, h, t

        def channel_column(u):
            return slice(u % (HALVES * PACK), u % (HALVES * PACK) + 1)

        def first_product(bank, h, t, codes, scales):
            cols = slice(P * (PACK * h + t), P * (PACK * h + t + 1))
            nc.tensor.matmul_mx(
                out=bank[:],
                lhsT=a_codes[:, cols].bitcast(FP8X4),
                lhsT_scale=a_scale_plane[:, cols],
                rhs=codes[:].bitcast(FP8X4),
                rhs_scale=scales[:],
                start=True,
                stop=True,
            )

        modulus = [None] * GROUPS

        def exponential(u):
            group, c, h, t = unit(u)
            if t == 0:
                modulus[group] = sbuf.tile([P, PACK, CHUNK], F32, name="modulus", bufs=GROUPS)
            q = psum.tile([P, CHUNK], F32, name="bank", bufs=3)
            first_product(q, h, t, *rho_codes[c])
            nc.scalar.activation(
                out=modulus[group][:, t, :], in_=q[:], func=ACT.Exp, bias=ln_g[:, channel_column(u)], scale=1.0
            )

        psi_bank = [None] * UNITS
        turns = [None] * UNITS
        angle = [None] * GROUPS
        cosine = [None] * GROUPS

        def psi_product(u):
            group, c, h, t = unit(u)
            psi_bank[u] = psum.tile([P, CHUNK], F32, name="psi", bufs=3)
            first_product(psi_bank[u], h, t, *theta_codes[c])

        def count_turns(u):
            turns[u] = sbuf.tile([P, CHUNK], I32, name="turns", bufs=3)
            nc.vector.tensor_scalar(
                out=turns[u][:],
                in0=psi_bank[u][:],
                scalar1=0.5 / PI,
                scalar2=phase_turns[:, channel_column(u)],
                op0=ALU.mult,
                op1=ALU.add,
            )

        def take_turns_off(u):
            group, c, h, t = unit(u)
            if t == 0:
                angle[group] = sbuf.tile([P, PACK, CHUNK], F32, name="angle", bufs=5)
            nc.vector.scalar_tensor_tensor(
                out=angle[group][:, t, :],
                in0=turns[u][:],
                scalar=-2 * PI,
                in1=psi_bank[u][:],
                op0=ALU.mult,
                op1=ALU.add,
            )

        def phase_step(u):
            if u == 0:
                psi_product(0)
            if u + 1 < UNITS:
                psi_product(u + 1)
            if u < UNITS:
                count_turns(u)
            if u > 0:
                take_turns_off(u - 1)

        def with_phase(target, group, func):
            for t in range(PACK):
                nc.scalar.activation(
                    out=target[:, t, :],
                    in_=angle[group][:, t, :],
                    func=func,
                    bias=phase[:, channel_column(PACK * group + t)],
                    scale=1.0,
                )

        def absolute(group):
            cosine[group] = sbuf.tile([P, PACK, CHUNK], F32, name="cosine", bufs=2)
            with_phase(cosine[group], group, ACT.Abs)

        def sine(group):
            with_phase(angle[group], group, ACT.Sin)

        def cosine_of_absolute(group, first=0, end=CHUNK):
            part = cosine[group][:, :, first:end]
            nc.scalar.activation(out=part, in_=part, func=ACT.Sin, bias=half_pi[:], scale=-1.0)

        product_packed = {}
        product_codes = {}

        def multiply(engine, group, w, first=0, end=CHUNK):
            if first == 0:
                product_packed[group, w] = sbuf.tile([P, CHUNK * PACK], BF16, name="packed_product", bufs=3, align_bytes=64)
            trig = (cosine, angle)[w][group]
            engine.tensor_tensor(
                out=product_packed[group, w][:, PACK * first : PACK * end].rearrange(
                    "p (c i t) -> p c t i", i=2, t=PACK
                ),
                in0=trig[:, :, first:end].rearrange("p t (c i) -> p c t i", i=2),
                in1=modulus[group][:, :, first:end].rearrange("p t (c i) -> p c t i", i=2),
                op=ALU.mult,
            )

        def multiply_shared(group, w):
            multiply(nc.vector, group, w, 0, VECTOR_COLS)
            multiply(nc.gpsimd, group, w, VECTOR_COLS, CHUNK)

        def quantise_product(group, w, first=0, end=CHUNK):
            if first == 0:
                product_codes[group, w] = (
                    sbuf.tile([P, CHUNK], U32, name="product_codes", bufs=6, align_bytes=64),
                    sbuf.tile([P, CHUNK], U8, name="product_scales", bufs=6, align_bytes=64),
                )
            codes, scales = product_codes[group, w]
            nc.vector.quantize_mx(
                out=codes[:, first:end].bitcast(FP8X4),
                scales=scales[:, first:end],
                in_=product_packed[group, w][:, PACK * first : PACK * end],
            )

        passes = ((0, SIN), (0, COS), (1, SIN), (1, COS))

        def output_passes(bank, c, r, which):
            cols = slice(P * r, P * (r + 1))
            for i in which:
                h, w = passes[i]
                codes, scales = product_codes[HALVES * c + h, w]
                plane = HALVES * w + h
                nc.tensor.matmul_mx(
                    out=bank[:],
                    lhsT=codes[:, cols].bitcast(FP8X4),
                    lhsT_scale=scales[:, cols],
                    rhs=w_codes[:, plane, :].bitcast(FP8X4),
                    rhs_scale=w_scales[4 * plane :, :],
                    start=(i == 0),
                    stop=(i == len(passes) - 1),
                )

        def store_output(bank, c, r, copy):
            rows = sbuf.tile([P, M], F32, name="out_rows", bufs=6)
            copy(out=rows[:], in_=bank[:])
            nc.sync.dma_start(out=out_rows[c][:, r, :], in_=rows[:])

        def output_bank(r, idle_ring, idle_bufs):
            if r < ROWS - 1:
                bank = psum.tile([P, M], F32, name="bank", bufs=3)
            else:
                bank = psum.tile([P, M], F32, name=idle_ring, bufs=idle_bufs)
            return bank

        spread_theta_scales()
        turn_rho(0)
        for r in range(ROWS):
            widen_theta(0, r)
        turn_theta(0)
        reorder_a()
        quantise_rho(0)
        load_rho(1)
        load_theta(1)
        load_theta(2)
        for r in range(ROWS):
            widen_theta(1, r)
        quantise_theta(0)

        for c in range(CHUNKS):
            for k in range(4):
                exponential(8 * c + 2 * k)
                exponential(8 * c + 2 * k + 1)
                if k == 0:
                    if c + 1 < CHUNKS:
                        turn_rho(c + 1)
                    continue
                if k == 1 and c > 0 and THETA_TURNED[c - 1] is not None:
                    quantise_theta(THETA_TURNED[c - 1])
                if k == 2 and THETA_TURNED[c] is not None:
                    turn_theta(THETA_TURNED[c])
                phase_step(3 * c + k - 1)
                if k == 2:
                    if c + 1 < CHUNKS:
                        quantise_rho(c + 1)
                    if c + 2 < CHUNKS:
                        load_rho(c + 2)
                elif THETA_WIDENED[c] is not None:
                    widen_theta(THETA_WIDENED[c], k - 1)
                    widen_theta(THETA_WIDENED[c], k)
                if c == 0 and k == 1:
                    load_output_weights()
                if c == 0 and k == 3:
                    load_theta(3)

        next_unit = 3 * CHUNKS
        for group in range(GROUPS):
            count = UNITS_BESIDE_SINES[group]
            units = list(range(next_unit, next_unit + count))
            next_unit += count
            c = (group - 3) // 2 if group >= 3 and group % 2 == 1 else None
            banks = []
            if group == 0:
                for u in units:
                    phase_step(u)
                quantise_theta(CHUNKS - 1)
            else:
                half = (count + 1) // 2
                for w, share, rows in ((SIN, units[:half], (0, 1)), (COS, units[half:], (2, 3))):
                    multiply_shared(group - 1, w)
                    for u in share[:1]:
                        phase_step(u)
                    if c is not None:
                        for r in rows:
                            banks.append(output_bank(r, "turn", 2))
                            output_passes(banks[r], c, r, range(4))
                    for u in share[1:]:
                        phase_step(u)
                quantise_product(group - 1, SIN)
                quantise_product(group - 1, COS)

            absolute(group)
            if c is not None:
                store_output(banks[0], c, 0, nc.scalar.copy)
            sine(group)
            if c is not None:
                store_output(banks[1], c, 1, nc.scalar.copy)
                store_output(banks[2], c, 2, nc.scalar.copy)
            quarters = 1 if group < GROUPS - 1 else 4
            for i in range(quarters):
                cosine_of_absolute(group, i * CHUNK // quarters, (i + 1) * CHUNK // quarters)
            if c is not None:
                store_output(banks[3], c, 3, nc.scalar.copy)

        group = GROUPS - 1
        c = CHUNKS - 1
        multiply(nc.vector, group, SIN)
        quantise_product(group, SIN)
        for r in range(ROWS + 1):
            if r < ROWS:
                multiply(nc.vector, group, COS, P * r, P * (r + 1))
            if r > 0:
                quantise_product(group, COS, P * (r - 1), P * r)
        banks = [output_bank(r, "psi", 3) for r in range(ROWS)]
        for which in ((0, 1), (2,)):
            for r in range(ROWS):
                output_passes(banks[r], c, r, which)
        for r in range(ROWS):
            output_passes(banks[r], c, r, (3,))
            store_output(banks[r], c, r, (nc.scalar.copy, nc.vector.tensor_copy)[r % 2])
